import numpy as np
import ml_dtypes


def mxq(x, axis, fmt="e4m3"):
    dtype, down = {"e4m3": (ml_dtypes.float8_e4m3fn, 7), "e5m2": (ml_dtypes.float8_e5m2, 14)}[fmt]
    v = np.moveaxis(np.asarray(x, np.float32).astype(ml_dtypes.bfloat16).astype(np.float64), axis, -1)
    blocks = v.reshape(v.shape[:-1] + (-1, 32))
    amax = np.abs(blocks).max(-1, keepdims=True)
    byte = np.maximum(np.where(amax > 0, np.frexp(amax)[1] - 1 + 127, 0) - down, 1)
    scale = np.exp2(byte - 127.0)
    codes = (blocks / scale).astype(np.float32).astype(dtype).astype(np.float64)
    return np.moveaxis((codes * scale).reshape(v.shape), -1, axis)


WIDE = False


def mx_kscale(k):
    if not WIDE:
        return np.ones(k)
    levels = np.array([10, -10, 5, -5, 0])
    if k % 512:
        return np.exp2(np.random.permutation(np.resize(levels, k // 32))).repeat(32)
    a = np.empty((k // 512, 16))
    for p in range(k // 512):
        a[p, :8] = np.random.permutation(np.resize(levels, 8))
        for g in range(8):
            far = levels[np.abs(levels - a[p, g]) >= 10]
            a[p, g + 8] = far[np.random.randint(len(far))]
    return np.exp2(a.ravel()).repeat(32)


def f64(x):
    return np.asarray(x).astype(np.float64)


def striped8(idx):
    return np.concatenate([x.reshape(-1, 16).T for x in idx]).astype(np.uint16)


def runs(offs, k):
    lists = np.stack([offs[16 * r : 16 * r + 16].T.reshape(-1) for r in range(8)]).astype(np.int64)
    return lists[np.arange(k) % 512 // 64]


def pack_weight(w):
    k, n = w.shape
    w = f64(np.asarray(w, np.float32).astype(ml_dtypes.bfloat16)).reshape(k // 32, 32, n)
    amax = np.abs(w).max(1)
    byte = np.clip(np.where(amax > 0, np.frexp(amax)[1] - 1 + 127 - 7, 1), 1, 254)
    scaled = (w * np.exp2(127.0 - byte)[:, None, :]).reshape(k, n).astype(np.float32)
    words = np.ascontiguousarray(scaled.reshape(k // 512, 128, 4, n).transpose(0, 1, 3, 2)).astype(ml_dtypes.float8_e4m3fn).view(np.uint8)
    return words, np.ascontiguousarray(byte.astype(np.uint8).reshape(k // 512, 16, n))


def unpack_weight(words, scales):
    g, p, n, _ = words.shape
    vals = np.ascontiguousarray(words).view(ml_dtypes.float8_e4m3fn).astype(np.float64) * np.repeat(np.exp2(scales.astype(np.float64) - 127.0), 8, axis=1)[..., None]
    return vals.transpose(0, 1, 3, 2).reshape(g * 512, n)


E2M1 = np.array([0.0, 0.5, 1.0, 1.5, 2.0, 3.0, 4.0, 6.0, -0.0, -0.5, -1.0, -1.5, -2.0, -3.0, -4.0, -6.0])


def pack_fp4(w):
    k, n = w.shape
    w = f64(np.asarray(w, np.float32).astype(ml_dtypes.bfloat16)).reshape(k // 32, 32, n)
    amax = np.abs(w).max(1)
    mant, ex = np.frexp(amax / 6.0)
    byte = np.clip(np.where(amax > 0, np.where(mant > 0.5, ex, ex - 1) + 127, 1), 1, 254)
    scaled = (w * np.exp2(127.0 - byte)[:, None, :]).reshape(k, n).astype(np.float32)
    c = np.ascontiguousarray(scaled.reshape(k // 512, 128, 4, n).transpose(0, 1, 3, 2)).astype(ml_dtypes.float4_e2m1fn).view(np.uint8) & 0xF
    words = (c[..., 0::2] | (c[..., 1::2] << 4)).reshape(k // 512, 128, 2 * n)
    return np.ascontiguousarray(words), np.ascontiguousarray(byte.astype(np.uint8).reshape(k // 512, 16, n))


def unpack_fp4(words, scales):
    g, _, n = scales.shape
    words = np.ascontiguousarray(words).reshape(g, 128, n, 2)
    nib = np.empty((g, 128, n, 4), np.uint8)
    nib[..., 0::2] = words & 0xF
    nib[..., 1::2] = words >> 4
    vals = E2M1[nib] * np.repeat(np.exp2(scales.astype(np.float64) - 127.0), 8, axis=1)[..., None]
    return vals.transpose(0, 1, 3, 2).reshape(g * 512, n)


def relu(v):
    return np.maximum(v, 0.0)

def planes(y):
    n, m = y.shape
    v = y.astype(np.float32).astype(ml_dtypes.bfloat16).astype(np.float64).reshape(n // 32, 32, m)
    top = np.abs(v).max(1)
    byte = np.clip(np.where(top > 0, np.frexp(top)[1] - 1 + 127 - 7, 1), 1, 254)
    codes = (v * np.exp2(127.0 - byte)[:, None, :]).reshape(n, m).astype(np.float32).astype(ml_dtypes.float8_e4m3fn).view(np.uint8)
    words = codes.reshape(n // 512, 128, 4, m).transpose(0, 1, 3, 2)
    return np.ascontiguousarray(words), np.ascontiguousarray(byte.astype(np.uint8).reshape(n // 512, 16, m))


K, T, S, N, H = 512, 2048, 512, 512, 512


def setup_inputs():
    n = np.random.standard_normal
    s = mx_kscale(K)[:, None]
    u = mx_kscale(H)
    packed_xT = pack_weight(n((K, T)) * s)
    packed_w1 = pack_fp4(n((K, H)) / np.sqrt(K) / s)
    packed_w2 = pack_fp4(n((H, N)) / np.sqrt(H) / u[:, None])
    return {
        "x_words": packed_xT[0],
        "x_scales": packed_xT[1],
        "w1_words": packed_w1[0],
        "w1_scales": packed_w1[1],
        "gn": (np.random.uniform(0.5, 1.5, (H, 1)) * u[:, None]).astype(np.float32),
        "w2_words": packed_w2[0],
        "w2_scales": packed_w2[1],
        "offs": striped8(np.random.randint(0, T, (8, S))),
        "n1": striped8(np.stack([np.random.permutation(S) for _ in range(8)])),
        "n2": striped8(np.stack([np.random.permutation(S) for _ in range(8)])),
        "n3": striped8(np.stack([np.random.permutation(S) for _ in range(8)])),
        "n4": striped8(np.stack([np.random.permutation(S) for _ in range(8)])),
    }


def reference(x_words, x_scales, w1_words, w1_scales, gn, w2_words, w2_scales, offs, n1, n2, n3, n4):
    xq = unpack_weight(x_words, x_scales)[np.arange(K)[:, None], runs(offs, K)]
    y = unpack_fp4(w1_words, w1_scales).T @ xq
    z = f64(gn) * (relu(y - (y[np.arange(H)[:, None], runs(n1, H)])) + 0.5 * (relu(y[np.arange(H)[:, None], runs(n2, H)] - y)))
    h = unpack_fp4(w2_words, w2_scales).T @ mxq(z, 0, "e4m3")
    out_0 = (h - (h[np.arange(N)[:, None], runs(n3, N)])) / (np.abs(h[np.arange(N)[:, None], runs(n4, N)] - h) + 0.5)
    return (out_0,) + planes(out_0)

@@ -1,0 +1,210 @@
+from contextlib import ExitStack
+
+import concourse.mybir as mybir
+
+K, T, S, N, H = 512, 2048, 512, 512, 512
+FLOPS = 2 * K * H * S + 2 * H * N * S
+
+F32 = mybir.dt.float32
+BF16 = mybir.dt.bfloat16
+I32 = mybir.dt.int32
+U32 = mybir.dt.uint32
+U16 = mybir.dt.uint16
+U8 = mybir.dt.uint8
+FP8X4 = mybir.dt.float8_e4m3fn_x4
+FP4X4 = mybir.dt.float4_e2m1fn_x4
+ALU = mybir.AluOpType
+ACT = mybir.ActivationFunctionType
+
+P = 128
+PACK = 4
+HALF = S // 2
+WHOLE_TILES = 2
+
+
+def tile_picked_hashhingefrac_none_po_kernel(
+    tc, x_words, x_scales, w1_words, w1_scales, gn, w2_words, w2_scales, offs, n1, n2, n3, n4, out_0, out_1, out_2
+):
+    nc = tc.nc
+    with ExitStack() as ctx:
+        keep = ctx.enter_context(tc.tile_pool(name="keep", bufs=1))
+        work = ctx.enter_context(tc.tile_pool(name="work", bufs=3))
+        psum = ctx.enter_context(tc.psum_pool(name="psum", bufs=1))
+
+        def held(shape, dtype, name):
+            return keep.tile(shape, dtype, name=name, align_bytes=64)
+
+        lists = {}
+        for name in ("offs", "n1", "n2", "n3", "n4"):
+            lists[name] = held([P, S // 16], U16, "list_" + name)
+
+        xs_table = held([P, T], U8, "xs_table")
+        nc.vector.memset(xs_table[:].bitcast(I32), 0)
+        nc.sync.dma_start(lists["offs"][:], offs)
+        for e in range(2):
+            nc.sync.dma_start(xs_table[e:P:16, :].bitcast(I32), x_scales[0, e:16:2, :].bitcast(I32))
+        xw_table = held([P, T], I32, "xw_table")
+        nc.sync.dma_start(xw_table[:], x_words[0].rearrange("p c r -> p (c r)").bitcast(I32))
+
+        ws_raw = [held([P, H], U8, "ws_raw%d" % i) for i in range(2)]
+        nc.gpsimd.memset(ws_raw[0][:].bitcast(I32), 0)
+        nc.vector.memset(ws_raw[1][:].bitcast(I32), 0)
+        w_raw = [held([P, 2 * H], U8, "w_raw%d" % i) for i in range(2)]
+        nc.sync.dma_start(w_raw[0][:].bitcast(I32), w1_words[0].bitcast(I32))
+
+        def load_scale_rows(queue, tile, rows, q):
+            queue.dma_start(tile[32 * q : 32 * q + 4, :].bitcast(I32), rows[0, 4 * q : 4 * q + 4, :].bitcast(I32))
+
+        for q in range(4):
+            load_scale_rows(nc.sync if q < 2 else nc.gpsimd, ws_raw[0], w1_scales, q)
+        nc.sync.dma_start(lists["n1"][:], n1)
+
+        warm = held([P, 1], F32, "warm")
+        nc.vector.memset(warm[:], 1.0)
+        warm_out = held([P, 1], F32, "warm_out")
+        nc.scalar.activation(warm_out[:], warm[:], ACT.Abs_reciprocal_sqrt)
+
+        windows = []
+        for t in range(PACK):
+            if t < WHOLE_TILES:
+                win = held([P, 2 * S], F32, "window%d" % t)
+                nc.vector.memset(win[:, S : 2 * S], 0.0)
+            else:
+                win = held([P, S], F32, "window%d" % t)
+            windows.append(win)
+        twins = [held([P, S], F32, "twin%d" % t) for t in range(PACK)]
+
+        xs_picked = held([P, S], U8, "xs_picked")
+        nc.vector.tensor_copy(xs_picked[:], xs_table[:].indirect(lists["offs"][:]))
+        xs_placed = held([P, S], U8, "xs_placed")
+        nc.vector.tensor_copy(xs_placed[:].bitcast(I32), xs_picked[:].bitcast(I32))
+        nc.sync.dma_start(xs_placed[2:P:32, :].bitcast(I32), xs_picked[16:P:32, :].bitcast(I32))
+        nc.scalar.dma_start(xs_placed[3:P:32, :].bitcast(I32), xs_picked[17:P:32, :].bitcast(I32))
+        nc.sync.dma_start(lists["n2"][:], n2)
+        gain = held([P, PACK], F32, "gain")
+        nc.sync.dma_start(gain[:], gn.rearrange("(p t) o -> p (t o)", t=PACK))
+        nc.sync.dma_start(w_raw[1][:].bitcast(I32), w2_words[0].bitcast(I32))
+        for q in range(4):
+            load_scale_rows(nc.sync, ws_raw[1], w2_scales, q)
+        nc.sync.dma_start(lists["n4"][:], n4)
+        nc.sync.dma_start(lists["n3"][:], n3)
+
+        def deal(i):
+            words = held([P, 2 * H], U8, "w_dealt%d" % i)
+            nc.vector.tensor_copy(
+                words[:].rearrange("p (t m b) -> p m t b", t=PACK, b=2),
+                w_raw[i][:].rearrange("p (m t b) -> p m t b", t=PACK, b=2),
+            )
+            scales = held([P, H], U8, "ws_dealt%d" % i)
+            nc.vector.tensor_copy(
+                scales[:].rearrange("p (t m) -> p m t", t=PACK),
+                ws_raw[i][:].rearrange("p (m t) -> p m t", t=PACK),
+            )
+            return words, scales
+
+        w1_dealt = deal(0)
+        xw_picked = held([P, S], U32, "xw_picked")
+        nc.vector.tensor_copy(xw_picked[:], xw_table[:].bitcast(U32).indirect(lists["offs"][:]))
+        w2_dealt = deal(1)
+        half_gain = held([P, PACK], F32, "half_gain")
+        nc.vector.tensor_scalar(half_gain[:], gain[:], 0.5, None, ALU.mult)
+
+        def product(bank, weights, t, codes, scales):
+            nc.tensor.matmul_mx(
+                out=bank,
+                lhsT=weights[0][:, 2 * P * t : 2 * P * (t + 1)].bitcast(FP4X4),
+                lhsT_scale=weights[1][:, P * t : P * (t + 1)],
+                rhs=codes.bitcast(FP8X4),
+                rhs_scale=scales,
+                start=True,
+                stop=True,
+            )
+
+        def less_self(name, t, lo, hi):
+            diff = work.tile([P, hi - lo], F32, name="diff_" + name)
+            nc.vector.tensor_tensor(
+                diff[:], windows[t][:].indirect(lists[name][:, lo // 16 : hi // 16]), twins[t][:, lo:hi], ALU.subtract
+            )
+            return diff
+
+        pieces = [(t, 0, S) for t in range(WHOLE_TILES)]
+        pieces = pieces + [(t, c * HALF, (c + 1) * HALF) for c in range(2) for t in range(WHOLE_TILES, PACK)]
+
+        def weave(engine_copy, woven, planes):
+            engine_copy(
+                woven[:].rearrange("p (c i t) -> p c t i", i=4, t=PACK),
+                planes[:].rearrange("p t (c i) -> p c t i", i=4),
+            )
+
+        banks = [psum.tile([P, S], F32, name="bank%d" % b) for b in range(8)]
+        for t in range(PACK):
+            product(banks[t][:], w1_dealt, t, xw_picked[:], xs_placed[:])
+        for t in range(PACK):
+            nc.scalar.copy(windows[t][:, 0:S], banks[t][:])
+            if t == 0:
+                nc.vector.tensor_copy(twins[t][:], windows[t][:, 0:S])
+            else:
+                nc.scalar.copy(twins[t][:], banks[t][:])
+
+        z_planes = [held([P, PACK, HALF], BF16, "z_planes%d" % c) for c in range(2)]
+        for t, lo, hi in pieces:
+            d1 = less_self("n1", t, lo, hi)
+            down = work.tile([P, hi - lo], F32, name="down")
+            nc.scalar.activation(down[:], d1[:], ACT.Relu, scale=-1.0)
+            d2 = less_self("n2", t, lo, hi)
+            up = work.tile([P, hi - lo], F32, name="up")
+            nc.vector.tensor_scalar(up[:], d2[:], 0.0, half_gain[:, t : t + 1], ALU.max, ALU.mult)
+            for c in range(lo // HALF, hi // HALF):
+                cols = slice(c * HALF - lo, (c + 1) * HALF - lo)
+                nc.vector.scalar_tensor_tensor(
+                    z_planes[c][:, t, :], down[:, cols], gain[:, t : t + 1], up[:, cols], ALU.mult, ALU.add
+                )
+            if t == PACK - 1:
+                c = lo // HALF
+                woven = held([P, PACK * HALF], BF16, "z_woven%d" % c)
+                weave(nc.scalar.copy if c == 0 else nc.vector.tensor_copy, woven, z_planes[c])
+                z_codes = held([P, HALF], U32, "z_codes%d" % c)
+                z_scales = held([P, HALF], U8, "z_scales%d" % c)
+                nc.vector.quantize_mx(out=z_codes[:].bitcast(FP8X4), scales=z_scales[:], in_=woven[:])
+                for u in range(PACK):
+                    product(banks[4 * (1 - c) + u][:, 0:HALF], w2_dealt, u, z_codes[:], z_scales[:])
+
+        for t in range(PACK):
+            for c in range(2):
+                cols = slice(c * HALF, (c + 1) * HALF)
+                bank = banks[4 * (1 - c) + t][:, 0:HALF]
+                nc.scalar.copy(windows[t][:, cols], bank)
+                if t == 0:
+                    nc.vector.tensor_copy(twins[t][:, cols], windows[t][:, cols])
+                else:
+                    nc.scalar.copy(twins[t][:, cols], bank)
+
+        out_rows = out_0.rearrange("(p t) j -> p t j", t=PACK)
+        out_words = out_1[0].rearrange("p c r -> p (c r)").bitcast(I32)
+        results = [held([P, PACK, HALF], F32, "result%d" % c) for c in range(2)]
+        o_scales = held([P, S], U8, "o_scales")
+        for t, lo, hi in pieces:
+            d4 = less_self("n4", t, lo, hi)
+            size = work.tile([P, hi - lo], F32, name="size")
+            nc.scalar.activation(size[:], d4[:], ACT.Abs)
+            root = work.tile([P, hi - lo], F32, name="root")
+            nc.scalar.activation(root[:], size[:], ACT.Abs_reciprocal_sqrt, bias=0.5)
+            inverse = work.tile([P, hi - lo], F32, name="inverse")
+            nc.scalar.activation(inverse[:], root[:], ACT.Square)
+            d3 = less_self("n3", t, lo, hi)
+            for c in range(lo // HALF, hi // HALF):
+                cols = slice(c * HALF - lo, (c + 1) * HALF - lo)
+                nc.vector.scalar_tensor_tensor(
+                    results[c][:, t, :], d3[:, cols], -1.0, inverse[:, cols], ALU.mult, ALU.mult
+                )
+                nc.sync.dma_start(out_rows[:, t, c * HALF : (c + 1) * HALF], results[c][:, t, :])
+            if t == PACK - 1:
+                c = lo // HALF
+                woven = held([P, PACK * HALF], BF16, "o_woven%d" % c)
+                weave(nc.scalar.copy if c == 0 else nc.vector.tensor_copy, woven, results[c])
+                o_codes = held([P, HALF], I32, "o_codes%d" % c)
+                nc.vector.quantize_mx(out=o_codes[:].bitcast(FP8X4), scales=o_scales[:, lo:hi], in_=woven[:])
+                nc.scalar.dma_start(out_words[:, lo:hi], o_codes[:])
+        for q in range(4):
+            queue = nc.sync if q % 2 == 0 else nc.scalar
+            queue.dma_start(out_2[0, 4 * q : 4 * q + 4, :].bitcast(I32), o_scales[32 * q : 32 * q + 4, :].bitcast(I32))

@@ -19,7 +19,9 @@ ACT = mybir.ActivationFunctionType
 P = 128
 PACK = 4
 HALF = S // 2
-WHOLE_TILES = 2
+CHUNKS = [(0, 256), (256, 384), (384, 512)]
+PIECES = [(0, 0, 512), (1, 0, 512), (2, 0, 256), (3, 0, 256), (2, 256, 512), (3, 256, 384), (3, 384, 512)]
+OUT_PIECES = [(0, 0, 512), (1, 0, 512), (2, 0, 256), (3, 0, 256), (2, 256, 512), (3, 256, 512)]
 
 
 def tile_picked_hashhingefrac_none_po_kernel(
@@ -38,76 +40,62 @@ def tile_picked_hashhingefrac_none_po_kernel(
         for name in ("offs", "n1", "n2", "n3", "n4"):
             lists[name] = held([P, S // 16], U16, "list_" + name)
 
+        def load_weights(words, scales):
+            raw_words = held([P, 2 * H], U8, "raw_words")
+            raw_scales = held([P, H], U8, "raw_scales")
+            nc.sync.dma_start(raw_words[:].bitcast(I32), words[0].bitcast(I32))
+            for q in range(4):
+                rows = scales[0, 4 * q : 4 * q + 4, :].bitcast(I32)
+                nc.sync.dma_start(raw_scales[32 * q : 32 * q + 32, :].bitcast(I32), rows.partition_broadcast(8))
+            return raw_words, raw_scales
+
         xs_table = held([P, T], U8, "xs_table")
-        nc.vector.memset(xs_table[:].bitcast(I32), 0)
+        nc.sync.dma_start(xs_table[:].bitcast(I32), x_scales[0].bitcast(I32).unsqueeze(1).to_broadcast([16, 8, T // 4]))
         nc.sync.dma_start(lists["offs"][:], offs)
-        for e in range(2):
-            nc.sync.dma_start(xs_table[e:P:16, :].bitcast(I32), x_scales[0, e:16:2, :].bitcast(I32))
+        w1_raw = load_weights(w1_words, w1_scales)
         xw_table = held([P, T], I32, "xw_table")
         nc.sync.dma_start(xw_table[:], x_words[0].rearrange("p c r -> p (c r)").bitcast(I32))
-
-        ws_raw = [held([P, H], U8, "ws_raw%d" % i) for i in range(2)]
-        nc.gpsimd.memset(ws_raw[0][:].bitcast(I32), 0)
-        nc.vector.memset(ws_raw[1][:].bitcast(I32), 0)
-        w_raw = [held([P, 2 * H], U8, "w_raw%d" % i) for i in range(2)]
-        nc.sync.dma_start(w_raw[0][:].bitcast(I32), w1_words[0].bitcast(I32))
-
-        def load_scale_rows(queue, tile, rows, q):
-            queue.dma_start(tile[32 * q : 32 * q + 4, :].bitcast(I32), rows[0, 4 * q : 4 * q + 4, :].bitcast(I32))
-
-        for q in range(4):
-            load_scale_rows(nc.sync if q < 2 else nc.gpsimd, ws_raw[0], w1_scales, q)
-        nc.sync.dma_start(lists["n1"][:], n1)
 
         warm = held([P, 1], F32, "warm")
         nc.vector.memset(warm[:], 1.0)
         warm_out = held([P, 1], F32, "warm_out")
         nc.scalar.activation(warm_out[:], warm[:], ACT.Abs_reciprocal_sqrt)
 
-        windows = []
-        for t in range(PACK):
-            if t < WHOLE_TILES:
-                win = held([P, 2 * S], F32, "window%d" % t)
+        def window(name, wide):
+            win = held([P, 2 * S if wide else S], F32, name)
+            if wide:
                 nc.vector.memset(win[:, S : 2 * S], 0.0)
-            else:
-                win = held([P, S], F32, "window%d" % t)
-            windows.append(win)
+            return win
+
+        windows = [window("window%d" % t, t < 2) for t in range(PACK)]
         twins = [held([P, S], F32, "twin%d" % t) for t in range(PACK)]
+        h_windows = windows[:2] + [window("h_window%d" % t, True) for t in (2, 3)]
+        h_twins = [held([P, S], F32, "h_twin%d" % t) for t in range(PACK)]
+        stage = {"n1": (windows, twins), "n2": (windows, twins), "n3": (h_windows, h_twins), "n4": (h_windows, h_twins)}
 
         xs_picked = held([P, S], U8, "xs_picked")
         nc.vector.tensor_copy(xs_picked[:], xs_table[:].indirect(lists["offs"][:]))
         xs_placed = held([P, S], U8, "xs_placed")
         nc.vector.tensor_copy(xs_placed[:].bitcast(I32), xs_picked[:].bitcast(I32))
-        nc.sync.dma_start(xs_placed[2:P:32, :].bitcast(I32), xs_picked[16:P:32, :].bitcast(I32))
-        nc.scalar.dma_start(xs_placed[3:P:32, :].bitcast(I32), xs_picked[17:P:32, :].bitcast(I32))
-        nc.sync.dma_start(lists["n2"][:], n2)
+        for i in range(1, 4):
+            nc.scalar.dma_start(xs_placed[i:P:32, :].bitcast(I32), xs_picked[8 * i : P : 32, :].bitcast(I32))
         gain = held([P, PACK], F32, "gain")
-        nc.sync.dma_start(gain[:], gn.rearrange("(p t) o -> p (t o)", t=PACK))
-        nc.sync.dma_start(w_raw[1][:].bitcast(I32), w2_words[0].bitcast(I32))
-        for q in range(4):
-            load_scale_rows(nc.sync, ws_raw[1], w2_scales, q)
-        nc.sync.dma_start(lists["n4"][:], n4)
-        nc.sync.dma_start(lists["n3"][:], n3)
+        nc.gpsimd.dma_start(gain[:], gn.rearrange("(p t) o -> p (t o)", t=PACK))
+        for name, source in (("n2", n2), ("n1", n1), ("n4", n4), ("n3", n3)):
+            nc.sync.dma_start(lists[name][:], source)
 
-        def deal(i):
-            words = held([P, 2 * H], U8, "w_dealt%d" % i)
+        def deal(raw, name):
+            words = held([P, 2 * H], U8, name + "_words")
             nc.vector.tensor_copy(
                 words[:].rearrange("p (t m b) -> p m t b", t=PACK, b=2),
-                w_raw[i][:].rearrange("p (m t b) -> p m t b", t=PACK, b=2),
+                raw[0][:].rearrange("p (m t b) -> p m t b", t=PACK, b=2),
             )
-            scales = held([P, H], U8, "ws_dealt%d" % i)
+            scales = held([P, H], U8, name + "_scales")
             nc.vector.tensor_copy(
                 scales[:].rearrange("p (t m) -> p m t", t=PACK),
-                ws_raw[i][:].rearrange("p (m t) -> p m t", t=PACK),
+                raw[1][:].rearrange("p (m t) -> p m t", t=PACK),
             )
             return words, scales
-
-        w1_dealt = deal(0)
-        xw_picked = held([P, S], U32, "xw_picked")
-        nc.vector.tensor_copy(xw_picked[:], xw_table[:].bitcast(U32).indirect(lists["offs"][:]))
-        w2_dealt = deal(1)
-        half_gain = held([P, PACK], F32, "half_gain")
-        nc.vector.tensor_scalar(half_gain[:], gain[:], 0.5, None, ALU.mult)
 
         def product(bank, weights, t, codes, scales):
             nc.tensor.matmul_mx(
@@ -120,15 +108,19 @@ def tile_picked_hashhingefrac_none_po_kernel(
                 stop=True,
             )
 
+        def leave_bank(engine_copy, name, t, lo, hi, bank):
+            engine_copy(stage[name][0][t][:, lo:hi], bank)
+            if t < 2:
+                engine_copy(stage[name][1][t][:, lo:hi], bank)
+            elif hi == S:
+                nc.sync.dma_start(stage[name][1][t][:], stage[name][0][t][:, 0:S])
+
         def less_self(name, t, lo, hi):
-            diff = work.tile([P, hi - lo], F32, name="diff_" + name)
+            diff = work.tile([P, hi - lo], F32, name="diff_" + name, bufs=2)
             nc.vector.tensor_tensor(
-                diff[:], windows[t][:].indirect(lists[name][:, lo // 16 : hi // 16]), twins[t][:, lo:hi], ALU.subtract
+                diff[:], stage[name][0][t][:].indirect(lists[name][:, lo // 16 : hi // 16]), stage[name][1][t][:, lo:hi], ALU.subtract
             )
             return diff
-
-        pieces = [(t, 0, S) for t in range(WHOLE_TILES)]
-        pieces = pieces + [(t, c * HALF, (c + 1) * HALF) for c in range(2) for t in range(WHOLE_TILES, PACK)]
 
         def weave(engine_copy, woven, planes):
             engine_copy(
@@ -136,75 +128,111 @@ def tile_picked_hashhingefrac_none_po_kernel(
                 planes[:].rearrange("p t (c i) -> p c t i", i=4),
             )
 
+        def chunks_in(lo, hi):
+            return [c for c in range(len(CHUNKS)) if lo <= CHUNKS[c][0] and CHUNKS[c][1] <= hi]
+
         banks = [psum.tile([P, S], F32, name="bank%d" % b) for b in range(8)]
-        for t in range(PACK):
-            product(banks[t][:], w1_dealt, t, xw_picked[:], xs_placed[:])
-        for t in range(PACK):
-            nc.scalar.copy(windows[t][:, 0:S], banks[t][:])
-            if t == 0:
-                nc.vector.tensor_copy(twins[t][:], windows[t][:, 0:S])
-            else:
-                nc.scalar.copy(twins[t][:], banks[t][:])
+        w1_dealt = deal(w1_raw, "w1")
+        w2_raw = load_weights(w2_words, w2_scales)
+        xw_picked = held([P, S], U32, "xw_picked")
+        for half in range(2):
+            lo, hi = half * HALF, (half + 1) * HALF
+            nc.vector.tensor_copy(xw_picked[:, lo:hi], xw_table[:].bitcast(U32).indirect(lists["offs"][:, lo // 16 : hi // 16]))
+            product(banks[half][:, 0:HALF], w1_dealt, 0, xw_picked[:, lo:hi], xs_placed[:, lo:hi])
+            leave_bank(nc.scalar.copy, "n1", 0, lo, hi, banks[half][:, 0:HALF])
+        for t in range(1, PACK):
+            product(banks[t + 1][:], w1_dealt, t, xw_picked[:], xs_placed[:])
+            leave_bank(nc.scalar.copy, "n1", t, 0, S, banks[t + 1][:])
+        w2_dealt = deal(w2_raw, "w2")
+        half_gain = held([P, PACK], F32, "half_gain")
+        nc.vector.tensor_scalar(half_gain[:], gain[:], 0.5, None, ALU.mult)
+        minus_gain = held([P, PACK], F32, "minus_gain")
+        nc.vector.tensor_scalar(minus_gain[:], gain[:], -1.0, None, ALU.mult)
 
-        z_planes = [held([P, PACK, HALF], BF16, "z_planes%d" % c) for c in range(2)]
-        for t, lo, hi in pieces:
-            d1 = less_self("n1", t, lo, hi)
-            down = work.tile([P, hi - lo], F32, name="down")
-            nc.scalar.activation(down[:], d1[:], ACT.Relu, scale=-1.0)
+        h_banks = [
+            [banks[5 + t // 2][:, HALF * (t % 2) : HALF * (t % 2 + 1)] for t in range(PACK)],
+            [banks[7][:, P * t : P * (t + 1)] for t in range(PACK)],
+            [banks[0][:, 0:P]] + [banks[1][:, P * t : P * (t + 1)] for t in range(1, PACK)],
+        ]
+        z_planes = [held([P, PACK, hi - lo], BF16, "z_planes%d" % lo) for lo, hi in CHUNKS]
+
+        def hinge_front(t, lo, hi):
+            if (t, lo, hi) == PIECES[-1]:
+                d1 = less_self("n1", t, lo, hi)
+                part = work.tile([P, hi - lo], F32, name="part")
+                nc.scalar.activation(part[:], d1[:], ACT.Relu, scale=-1.0)
+                return part, less_self("n2", t, lo, hi)
             d2 = less_self("n2", t, lo, hi)
-            up = work.tile([P, hi - lo], F32, name="up")
-            nc.vector.tensor_scalar(up[:], d2[:], 0.0, half_gain[:, t : t + 1], ALU.max, ALU.mult)
-            for c in range(lo // HALF, hi // HALF):
-                cols = slice(c * HALF - lo, (c + 1) * HALF - lo)
-                nc.vector.scalar_tensor_tensor(
-                    z_planes[c][:, t, :], down[:, cols], gain[:, t : t + 1], up[:, cols], ALU.mult, ALU.add
-                )
-            if t == PACK - 1:
-                c = lo // HALF
-                woven = held([P, PACK * HALF], BF16, "z_woven%d" % c)
-                weave(nc.scalar.copy if c == 0 else nc.vector.tensor_copy, woven, z_planes[c])
-                z_codes = held([P, HALF], U32, "z_codes%d" % c)
-                z_scales = held([P, HALF], U8, "z_scales%d" % c)
-                nc.vector.quantize_mx(out=z_codes[:].bitcast(FP8X4), scales=z_scales[:], in_=woven[:])
-                for u in range(PACK):
-                    product(banks[4 * (1 - c) + u][:, 0:HALF], w2_dealt, u, z_codes[:], z_scales[:])
+            part = work.tile([P, hi - lo], F32, name="part")
+            nc.scalar.activation(part[:], d2[:], ACT.Relu, scale=0.5)
+            return part, less_self("n1", t, lo, hi)
+
+        def hinge_back(t, lo, hi, part, diff):
+            both = work.tile([P, hi - lo], F32, name="both")
+            last = (t, lo, hi) == PIECES[-1]
+            if last:
+                nc.vector.tensor_scalar(both[:], diff[:], 0.0, half_gain[:, t : t + 1], ALU.max, ALU.mult)
+                nc.vector.scalar_tensor_tensor(z_planes[-1][:, t, :], part[:], gain[:, t : t + 1], both[:], ALU.mult, ALU.add)
+            else:
+                nc.vector.scalar_tensor_tensor(both[:], diff[:], 0.0, part[:], ALU.min, ALU.subtract)
+            for c in chunks_in(lo, hi):
+                clo, chi = CHUNKS[c]
+                if not last:
+                    nc.scalar.activation(z_planes[c][:, t, :], both[:, clo - lo : chi - lo], ACT.Copy, scale=minus_gain[:, t : t + 1])
+                if t == PACK - 1:
+                    woven = held([P, PACK * (chi - clo)], BF16, "z_woven%d" % c)
+                    weave(nc.vector.tensor_copy if last else nc.scalar.copy, woven, z_planes[c])
+                    z_codes = held([P, chi - clo], U32, "z_codes%d" % c)
+                    z_scales = held([P, chi - clo], U8, "z_scales%d" % c)
+                    nc.vector.quantize_mx(out=z_codes[:].bitcast(FP8X4), scales=z_scales[:], in_=woven[:])
+                    for u in range(PACK):
+                        product(h_banks[c][u], w2_dealt, u, z_codes[:], z_scales[:])
+
+        for t, lo, hi in PIECES:
+            part, diff = hinge_front(t, lo, hi)
+            hinge_back(t, lo, hi, part, diff)
 
         for t in range(PACK):
-            for c in range(2):
-                cols = slice(c * HALF, (c + 1) * HALF)
-                bank = banks[4 * (1 - c) + t][:, 0:HALF]
-                nc.scalar.copy(windows[t][:, cols], bank)
-                if t == 0:
-                    nc.vector.tensor_copy(twins[t][:, cols], windows[t][:, cols])
-                else:
-                    nc.scalar.copy(twins[t][:, cols], bank)
+            for c in range(len(CHUNKS)):
+                on_vector = t == 0 and c == len(CHUNKS) - 1
+                leave_bank(nc.vector.tensor_copy if on_vector else nc.scalar.copy, "n3", t, CHUNKS[c][0], CHUNKS[c][1], h_banks[c][t])
 
         out_rows = out_0.rearrange("(p t) j -> p t j", t=PACK)
         out_words = out_1[0].rearrange("p c r -> p (c r)").bitcast(I32)
         results = [held([P, PACK, HALF], F32, "result%d" % c) for c in range(2)]
         o_scales = held([P, S], U8, "o_scales")
-        for t, lo, hi in pieces:
-            d4 = less_self("n4", t, lo, hi)
-            size = work.tile([P, hi - lo], F32, name="size")
+        inverses = []
+
+        def denominator(t):
+            d4 = less_self("n4", t, 0, S)
+            size = work.tile([P, S], F32, name="size")
             nc.scalar.activation(size[:], d4[:], ACT.Abs)
-            root = work.tile([P, hi - lo], F32, name="root")
+            root = work.tile([P, S], F32, name="root")
             nc.scalar.activation(root[:], size[:], ACT.Abs_reciprocal_sqrt, bias=0.5)
-            inverse = work.tile([P, hi - lo], F32, name="inverse")
+            inverse = held([P, S], F32, "inverse%d" % t)
             nc.scalar.activation(inverse[:], root[:], ACT.Square)
+            inverses.append(inverse)
+
+        denominator(0)
+        for t, lo, hi in OUT_PIECES:
+            if lo == 0 and t + 1 < PACK:
+                denominator(t + 1)
             d3 = less_self("n3", t, lo, hi)
             for c in range(lo // HALF, hi // HALF):
-                cols = slice(c * HALF - lo, (c + 1) * HALF - lo)
+                clo, chi = c * HALF, (c + 1) * HALF
                 nc.vector.scalar_tensor_tensor(
-                    results[c][:, t, :], d3[:, cols], -1.0, inverse[:, cols], ALU.mult, ALU.mult
+                    results[c][:, t, :], d3[:, clo - lo : chi - lo], -1.0, inverses[t][:, clo:chi], ALU.mult, ALU.mult
                 )
-                nc.sync.dma_start(out_rows[:, t, c * HALF : (c + 1) * HALF], results[c][:, t, :])
-            if t == PACK - 1:
-                c = lo // HALF
-                woven = held([P, PACK * HALF], BF16, "o_woven%d" % c)
-                weave(nc.scalar.copy if c == 0 else nc.vector.tensor_copy, woven, results[c])
-                o_codes = held([P, HALF], I32, "o_codes%d" % c)
-                nc.vector.quantize_mx(out=o_codes[:].bitcast(FP8X4), scales=o_scales[:, lo:hi], in_=woven[:])
-                nc.scalar.dma_start(out_words[:, lo:hi], o_codes[:])
+                if t == 1:
+                    nc.sync.dma_start(out_rows[:, 0:2, clo:chi], results[c][:, 0:2, :])
+                if t > 1:
+                    nc.sync.dma_start(out_rows[:, t, clo:chi], results[c][:, t, :])
+                if t == PACK - 1:
+                    woven = held([P, PACK * HALF], BF16, "o_woven%d" % c)
+                    weave(nc.vector.tensor_copy if chi == S else nc.scalar.copy, woven, results[c])
+                    o_codes = held([P, HALF], I32, "o_codes%d" % c)
+                    nc.vector.quantize_mx(out=o_codes[:].bitcast(FP8X4), scales=o_scales[:, clo:chi], in_=woven[:])
+                    nc.scalar.dma_start(out_words[:, clo:chi], o_codes[:])
         for q in range(4):
             queue = nc.sync if q % 2 == 0 else nc.scalar
             queue.dma_start(out_2[0, 4 * q : 4 * q + 4, :].bitcast(I32), o_scales[32 * q : 32 * q + 4, :].bitcast(I32))

@@ -40,19 +40,19 @@ def tile_picked_hashhingefrac_none_po_kernel(
         for name in ("offs", "n1", "n2", "n3", "n4"):
             lists[name] = held([P, S // 16], U16, "list_" + name)
 
-        def load_weights(words, scales):
-            raw_words = held([P, 2 * H], U8, "raw_words")
-            raw_scales = held([P, H], U8, "raw_scales")
-            nc.sync.dma_start(raw_words[:].bitcast(I32), words[0].bitcast(I32))
+        def load_weights(words, scales, name):
+            raw = held([P, 3 * H], U8, name)
+            raw_words, raw_scales = raw[:, 0 : 2 * H], raw[:, 2 * H : 3 * H]
+            nc.sync.dma_start(raw_words.bitcast(I32), words[0].bitcast(I32))
             for q in range(4):
                 rows = scales[0, 4 * q : 4 * q + 4, :].bitcast(I32)
                 nc.sync.dma_start(raw_scales[32 * q : 32 * q + 32, :].bitcast(I32), rows.partition_broadcast(8))
             return raw_words, raw_scales
 
-        xs_table = held([P, T], U8, "xs_table")
+        xs_table = held([P, T], U8, "staging")
         nc.sync.dma_start(xs_table[:].bitcast(I32), x_scales[0].bitcast(I32).unsqueeze(1).to_broadcast([16, 8, T // 4]))
         nc.sync.dma_start(lists["offs"][:], offs)
-        w1_raw = load_weights(w1_words, w1_scales)
+        w1_raw = load_weights(w1_words, w1_scales, "w1_raw")
         xw_table = held([P, T], I32, "xw_table")
         nc.sync.dma_start(xw_table[:], x_words[0].rearrange("p c r -> p (c r)").bitcast(I32))
 
@@ -79,6 +79,7 @@ def tile_picked_hashhingefrac_none_po_kernel(
         nc.vector.tensor_copy(xs_placed[:].bitcast(I32), xs_picked[:].bitcast(I32))
         for i in range(1, 4):
             nc.scalar.dma_start(xs_placed[i:P:32, :].bitcast(I32), xs_picked[8 * i : P : 32, :].bitcast(I32))
+        w2_raw = load_weights(w2_words, w2_scales, "staging")
         gain = held([P, PACK], F32, "gain")
         nc.gpsimd.dma_start(gain[:], gn.rearrange("(p t) o -> p (t o)", t=PACK))
         for name, source in (("n2", n2), ("n1", n1), ("n4", n4), ("n3", n3)):
@@ -88,12 +89,12 @@ def tile_picked_hashhingefrac_none_po_kernel(
             words = held([P, 2 * H], U8, name + "_words")
             nc.vector.tensor_copy(
                 words[:].rearrange("p (t m b) -> p m t b", t=PACK, b=2),
-                raw[0][:].rearrange("p (m t b) -> p m t b", t=PACK, b=2),
+                raw[0].rearrange("p (m t b) -> p m t b", t=PACK, b=2),
             )
             scales = held([P, H], U8, name + "_scales")
             nc.vector.tensor_copy(
                 scales[:].rearrange("p (t m) -> p m t", t=PACK),
-                raw[1][:].rearrange("p (m t) -> p m t", t=PACK),
+                raw[1].rearrange("p (m t) -> p m t", t=PACK),
             )
             return words, scales
 
@@ -125,7 +126,7 @@ def tile_picked_hashhingefrac_none_po_kernel(
         def weave(engine_copy, woven, planes):
             engine_copy(
                 woven[:].rearrange("p (c i t) -> p c t i", i=4, t=PACK),
-                planes[:].rearrange("p t (c i) -> p c t i", i=4),
+                planes.rearrange("p t (c i) -> p c t i", i=4),
             )
 
         def chunks_in(lo, hi):
@@ -133,21 +134,20 @@ def tile_picked_hashhingefrac_none_po_kernel(
 
         banks = [psum.tile([P, S], F32, name="bank%d" % b) for b in range(8)]
         w1_dealt = deal(w1_raw, "w1")
-        w2_raw = load_weights(w2_words, w2_scales)
         xw_picked = held([P, S], U32, "xw_picked")
         for half in range(2):
             lo, hi = half * HALF, (half + 1) * HALF
             nc.vector.tensor_copy(xw_picked[:, lo:hi], xw_table[:].bitcast(U32).indirect(lists["offs"][:, lo // 16 : hi // 16]))
             product(banks[half][:, 0:HALF], w1_dealt, 0, xw_picked[:, lo:hi], xs_placed[:, lo:hi])
-            leave_bank(nc.scalar.copy, "n1", 0, lo, hi, banks[half][:, 0:HALF])
+            leave_bank(nc.vector.tensor_copy if half else nc.scalar.copy, "n1", 0, lo, hi, banks[half][:, 0:HALF])
         for t in range(1, PACK):
             product(banks[t + 1][:], w1_dealt, t, xw_picked[:], xs_placed[:])
             leave_bank(nc.scalar.copy, "n1", t, 0, S, banks[t + 1][:])
         w2_dealt = deal(w2_raw, "w2")
         half_gain = held([P, PACK], F32, "half_gain")
-        nc.vector.tensor_scalar(half_gain[:], gain[:], 0.5, None, ALU.mult)
+        nc.scalar.activation(half_gain[:], gain[:], ACT.Copy, scale=0.5)
         minus_gain = held([P, PACK], F32, "minus_gain")
-        nc.vector.tensor_scalar(minus_gain[:], gain[:], -1.0, None, ALU.mult)
+        nc.scalar.activation(minus_gain[:], gain[:], ACT.Copy, scale=-1.0)
 
         h_banks = [
             [banks[5 + t // 2][:, HALF * (t % 2) : HALF * (t % 2 + 1)] for t in range(PACK)],
@@ -158,10 +158,11 @@ def tile_picked_hashhingefrac_none_po_kernel(
 
         def hinge_front(t, lo, hi):
             if (t, lo, hi) == PIECES[-1]:
+                d2 = less_self("n2", t, lo, hi)
                 d1 = less_self("n1", t, lo, hi)
                 part = work.tile([P, hi - lo], F32, name="part")
                 nc.scalar.activation(part[:], d1[:], ACT.Relu, scale=-1.0)
-                return part, less_self("n2", t, lo, hi)
+                return part, d2
             d2 = less_self("n2", t, lo, hi)
             part = work.tile([P, hi - lo], F32, name="part")
             nc.scalar.activation(part[:], d2[:], ACT.Relu, scale=0.5)
@@ -181,7 +182,7 @@ def tile_picked_hashhingefrac_none_po_kernel(
                     nc.scalar.activation(z_planes[c][:, t, :], both[:, clo - lo : chi - lo], ACT.Copy, scale=minus_gain[:, t : t + 1])
                 if t == PACK - 1:
                     woven = held([P, PACK * (chi - clo)], BF16, "z_woven%d" % c)
-                    weave(nc.vector.tensor_copy if last else nc.scalar.copy, woven, z_planes[c])
+                    weave(nc.vector.tensor_copy if last else nc.scalar.copy, woven, z_planes[c][:])
                     z_codes = held([P, chi - clo], U32, "z_codes%d" % c)
                     z_scales = held([P, chi - clo], U8, "z_scales%d" % c)
                     nc.vector.quantize_mx(out=z_codes[:].bitcast(FP8X4), scales=z_scales[:], in_=woven[:])
@@ -199,7 +200,7 @@ def tile_picked_hashhingefrac_none_po_kernel(
 
         out_rows = out_0.rearrange("(p t) j -> p t j", t=PACK)
         out_words = out_1[0].rearrange("p c r -> p (c r)").bitcast(I32)
-        results = [held([P, PACK, HALF], F32, "result%d" % c) for c in range(2)]
+        result = held([P, PACK, S], F32, "result")
         o_scales = held([P, S], U8, "o_scales")
         inverses = []
 
@@ -218,21 +219,14 @@ def tile_picked_hashhingefrac_none_po_kernel(
             if lo == 0 and t + 1 < PACK:
                 denominator(t + 1)
             d3 = less_self("n3", t, lo, hi)
-            for c in range(lo // HALF, hi // HALF):
-                clo, chi = c * HALF, (c + 1) * HALF
-                nc.vector.scalar_tensor_tensor(
-                    results[c][:, t, :], d3[:, clo - lo : chi - lo], -1.0, inverses[t][:, clo:chi], ALU.mult, ALU.mult
-                )
-                if t == 1:
-                    nc.sync.dma_start(out_rows[:, 0:2, clo:chi], results[c][:, 0:2, :])
-                if t > 1:
-                    nc.sync.dma_start(out_rows[:, t, clo:chi], results[c][:, t, :])
-                if t == PACK - 1:
-                    woven = held([P, PACK * HALF], BF16, "o_woven%d" % c)
-                    weave(nc.vector.tensor_copy if chi == S else nc.scalar.copy, woven, results[c])
-                    o_codes = held([P, HALF], I32, "o_codes%d" % c)
-                    nc.vector.quantize_mx(out=o_codes[:].bitcast(FP8X4), scales=o_scales[:, clo:chi], in_=woven[:])
-                    nc.scalar.dma_start(out_words[:, clo:chi], o_codes[:])
+            nc.vector.scalar_tensor_tensor(result[:, t, lo:hi], d3[:], -1.0, inverses[t][:, lo:hi], ALU.mult, ALU.mult)
+            nc.sync.dma_start(out_rows[:, t, lo:hi], result[:, t, lo:hi])
+            if t == PACK - 1:
+                woven = held([P, PACK * HALF], BF16, "o_woven%d" % lo)
+                weave(nc.vector.tensor_copy if hi == S else nc.scalar.copy, woven, result[:, :, lo:hi])
+                o_codes = held([P, HALF], I32, "o_codes%d" % lo)
+                nc.vector.quantize_mx(out=o_codes[:].bitcast(FP8X4), scales=o_scales[:, lo:hi], in_=woven[:])
+                nc.scalar.dma_start(out_words[:, lo:hi], o_codes[:])
         for q in range(4):
             queue = nc.sync if q % 2 == 0 else nc.scalar
             queue.dma_start(out_2[0, 4 * q : 4 * q + 4, :].bitcast(I32), o_scales[32 * q : 32 * q + 4, :].bitcast(I32))

@@ -117,7 +117,7 @@ def tile_picked_hashhingefrac_none_po_kernel(
                 nc.sync.dma_start(stage[name][1][t][:], stage[name][0][t][:, 0:S])
 
         def less_self(name, t, lo, hi):
-            diff = work.tile([P, hi - lo], F32, name="diff_" + name, bufs=2)
+            diff = work.tile([P, hi - lo], F32, name="diff_" + name, bufs=3)
             nc.vector.tensor_tensor(
                 diff[:], stage[name][0][t][:].indirect(lists[name][:, lo // 16 : hi // 16]), stage[name][1][t][:, lo:hi], ALU.subtract
             )
@@ -182,7 +182,7 @@ def tile_picked_hashhingefrac_none_po_kernel(
                     nc.scalar.activation(z_planes[c][:, t, :], both[:, clo - lo : chi - lo], ACT.Copy, scale=minus_gain[:, t : t + 1])
                 if t == PACK - 1:
                     woven = held([P, PACK * (chi - clo)], BF16, "z_woven%d" % c)
-                    weave(nc.vector.tensor_copy if last else nc.scalar.copy, woven, z_planes[c][:])
+                    weave(nc.vector.tensor_copy if c > 0 else nc.scalar.copy, woven, z_planes[c][:])
                     z_codes = held([P, chi - clo], U32, "z_codes%d" % c)
                     z_scales = held([P, chi - clo], U8, "z_scales%d" % c)
                     nc.vector.quantize_mx(out=z_codes[:].bitcast(FP8X4), scales=z_scales[:], in_=woven[:])

from contextlib import ExitStack

import concourse.mybir as mybir

K, T, S, N, H = 512, 2048, 512, 512, 512
FLOPS = 2 * K * H * S + 2 * H * N * S

F32 = mybir.dt.float32
BF16 = mybir.dt.bfloat16
I32 = mybir.dt.int32
U32 = mybir.dt.uint32
U16 = mybir.dt.uint16
U8 = mybir.dt.uint8
FP8X4 = mybir.dt.float8_e4m3fn_x4
FP4X4 = mybir.dt.float4_e2m1fn_x4
ALU = mybir.AluOpType
ACT = mybir.ActivationFunctionType

P = 128
PACK = 4
HALF = S // 2
CHUNKS = [(0, 256), (256, 384), (384, 512)]
PIECES = [(0, 0, 512), (1, 0, 512), (2, 0, 256), (3, 0, 256), (2, 256, 512), (3, 256, 384), (3, 384, 512)]
OUT_PIECES = [(0, 0, 512), (1, 0, 512), (2, 0, 256), (3, 0, 256), (2, 256, 512), (3, 256, 512)]


def tile_picked_hashhingefrac_none_po_kernel(
    tc, x_words, x_scales, w1_words, w1_scales, gn, w2_words, w2_scales, offs, n1, n2, n3, n4, out_0, out_1, out_2
):
    nc = tc.nc
    with ExitStack() as ctx:
        keep = ctx.enter_context(tc.tile_pool(name="keep", bufs=1))
        work = ctx.enter_context(tc.tile_pool(name="work", bufs=3))
        psum = ctx.enter_context(tc.psum_pool(name="psum", bufs=1))

        def held(shape, dtype, name):
            return keep.tile(shape, dtype, name=name, align_bytes=64)

        lists = {}
        for name in ("offs", "n1", "n2", "n3", "n4"):
            lists[name] = held([P, S // 16], U16, "list_" + name)

        def load_weights(words, scales, name):
            raw = held([P, 3 * H], U8, name)
            raw_words, raw_scales = raw[:, 0 : 2 * H], raw[:, 2 * H : 3 * H]
            nc.sync.dma_start(raw_words.bitcast(I32), words[0].bitcast(I32))
            for q in range(4):
                rows = scales[0, 4 * q : 4 * q + 4, :].bitcast(I32)
                nc.sync.dma_start(raw_scales[32 * q : 32 * q + 32, :].bitcast(I32), rows.partition_broadcast(8))
            return raw_words, raw_scales

        xs_table = held([P, T], U8, "staging")
        nc.sync.dma_start(xs_table[:].bitcast(I32), x_scales[0].bitcast(I32).unsqueeze(1).to_broadcast([16, 8, T // 4]))
        nc.sync.dma_start(lists["offs"][:], offs)
        w1_raw = load_weights(w1_words, w1_scales, "w1_raw")
        xw_table = held([P, T], I32, "xw_table")
        nc.sync.dma_start(xw_table[:], x_words[0].rearrange("p c r -> p (c r)").bitcast(I32))

        warm = held([P, 1], F32, "warm")
        nc.vector.memset(warm[:], 1.0)
        warm_out = held([P, 1], F32, "warm_out")
        nc.scalar.activation(warm_out[:], warm[:], ACT.Abs_reciprocal_sqrt)

        def window(name, wide):
            win = held([P, 2 * S if wide else S], F32, name)
            if wide:
                nc.vector.memset(win[:, S : 2 * S], 0.0)
            return win

        windows = [window("window%d" % t, t < 2) for t in range(PACK)]
        twins = [held([P, S], F32, "twin%d" % t) for t in range(PACK)]
        h_windows = windows[:2] + [window("h_window%d" % t, True) for t in (2, 3)]
        h_twins = [held([P, S], F32, "h_twin%d" % t) for t in range(PACK)]
        stage = {"n1": (windows, twins), "n2": (windows, twins), "n3": (h_windows, h_twins), "n4": (h_windows, h_twins)}

        xs_picked = held([P, S], U8, "xs_picked")
        nc.vector.tensor_copy(xs_picked[:], xs_table[:].indirect(lists["offs"][:]))
        xs_placed = held([P, S], U8, "xs_placed")
        nc.vector.tensor_copy(xs_placed[:].bitcast(I32), xs_picked[:].bitcast(I32))
        for i in range(1, 4):
            nc.scalar.dma_start(xs_placed[i:P:32, :].bitcast(I32), xs_picked[8 * i : P : 32, :].bitcast(I32))
        w2_raw = load_weights(w2_words, w2_scales, "staging")
        gain = held([P, PACK], F32, "gain")
        nc.gpsimd.dma_start(gain[:], gn.rearrange("(p t) o -> p (t o)", t=PACK))
        for name, source in (("n2", n2), ("n1", n1), ("n4", n4), ("n3", n3)):
            nc.sync.dma_start(lists[name][:], source)

        def deal(raw, name):
            words = held([P, 2 * H], U8, name + "_words")
            nc.vector.tensor_copy(
                words[:].rearrange("p (t m b) -> p m t b", t=PACK, b=2),
                raw[0].rearrange("p (m t b) -> p m t b", t=PACK, b=2),
            )
            scales = held([P, H], U8, name + "_scales")
            nc.vector.tensor_copy(
                scales[:].rearrange("p (t m) -> p m t", t=PACK),
                raw[1].rearrange("p (m t) -> p m t", t=PACK),
            )
            return words, scales

        def product(bank, weights, t, codes, scales):
            nc.tensor.matmul_mx(
                out=bank,
                lhsT=weights[0][:, 2 * P * t : 2 * P * (t + 1)].bitcast(FP4X4),
                lhsT_scale=weights[1][:, P * t : P * (t + 1)],
                rhs=codes.bitcast(FP8X4),
                rhs_scale=scales,
                start=True,
                stop=True,
            )

        def leave_bank(engine_copy, name, t, lo, hi, bank):
            engine_copy(stage[name][0][t][:, lo:hi], bank)
            if t < 2:
                engine_copy(stage[name][1][t][:, lo:hi], bank)
            elif hi == S:
                nc.sync.dma_start(stage[name][1][t][:], stage[name][0][t][:, 0:S])

        def less_self(name, t, lo, hi):
            diff = work.tile([P, hi - lo], F32, name="diff_" + name, bufs=3)
            nc.vector.tensor_tensor(
                diff[:], stage[name][0][t][:].indirect(lists[name][:, lo // 16 : hi // 16]), stage[name][1][t][:, lo:hi], ALU.subtract
            )
            return diff

        def weave(engine_copy, woven, planes):
            engine_copy(
                woven[:].rearrange("p (c i t) -> p c t i", i=4, t=PACK),
                planes.rearrange("p t (c i) -> p c t i", i=4),
            )

        def chunks_in(lo, hi):
            return [c for c in range(len(CHUNKS)) if lo <= CHUNKS[c][0] and CHUNKS[c][1] <= hi]

        banks = [psum.tile([P, S], F32, name="bank%d" % b) for b in range(8)]
        w1_dealt = deal(w1_raw, "w1")
        xw_picked = held([P, S], U32, "xw_picked")
        for half in range(2):
            lo, hi = half * HALF, (half + 1) * HALF
            nc.vector.tensor_copy(xw_picked[:, lo:hi], xw_table[:].bitcast(U32).indirect(lists["offs"][:, lo // 16 : hi // 16]))
            product(banks[half][:, 0:HALF], w1_dealt, 0, xw_picked[:, lo:hi], xs_placed[:, lo:hi])
            leave_bank(nc.vector.tensor_copy if half else nc.scalar.copy, "n1", 0, lo, hi, banks[half][:, 0:HALF])
        for t in range(1, PACK):
            product(banks[t + 1][:], w1_dealt, t, xw_picked[:], xs_placed[:])
            leave_bank(nc.scalar.copy, "n1", t, 0, S, banks[t + 1][:])
        w2_dealt = deal(w2_raw, "w2")
        half_gain = held([P, PACK], F32, "half_gain")
        nc.scalar.activation(half_gain[:], gain[:], ACT.Copy, scale=0.5)
        minus_gain = held([P, PACK], F32, "minus_gain")
        nc.scalar.activation(minus_gain[:], gain[:], ACT.Copy, scale=-1.0)

        h_banks = [
            [banks[5 + t // 2][:, HALF * (t % 2) : HALF * (t % 2 + 1)] for t in range(PACK)],
            [banks[7][:, P * t : P * (t + 1)] for t in range(PACK)],
            [banks[0][:, 0:P]] + [banks[1][:, P * t : P * (t + 1)] for t in range(1, PACK)],
        ]
        z_planes = [held([P, PACK, hi - lo], BF16, "z_planes%d" % lo) for lo, hi in CHUNKS]

        def hinge_front(t, lo, hi):
            if (t, lo, hi) == PIECES[-1]:
                d2 = less_self("n2", t, lo, hi)
                d1 = less_self("n1", t, lo, hi)
                part = work.tile([P, hi - lo], F32, name="part")
                nc.scalar.activation(part[:], d1[:], ACT.Relu, scale=-1.0)
                return part, d2
            d2 = less_self("n2", t, lo, hi)
            part = work.tile([P, hi - lo], F32, name="part")
            nc.scalar.activation(part[:], d2[:], ACT.Relu, scale=0.5)
            return part, less_self("n1", t, lo, hi)

        def hinge_back(t, lo, hi, part, diff):
            both = work.tile([P, hi - lo], F32, name="both")
            last = (t, lo, hi) == PIECES[-1]
            if last:
                nc.vector.tensor_scalar(both[:], diff[:], 0.0, half_gain[:, t : t + 1], ALU.max, ALU.mult)
                nc.vector.scalar_tensor_tensor(z_planes[-1][:, t, :], part[:], gain[:, t : t + 1], both[:], ALU.mult, ALU.add)
            else:
                nc.vector.scalar_tensor_tensor(both[:], diff[:], 0.0, part[:], ALU.min, ALU.subtract)
            for c in chunks_in(lo, hi):
                clo, chi = CHUNKS[c]
                if not last:
                    nc.scalar.activation(z_planes[c][:, t, :], both[:, clo - lo : chi - lo], ACT.Copy, scale=minus_gain[:, t : t + 1])
                if t == PACK - 1:
                    woven = held([P, PACK * (chi - clo)], BF16, "z_woven%d" % c)
                    weave(nc.vector.tensor_copy if c > 0 else nc.scalar.copy, woven, z_planes[c][:])
                    z_codes = held([P, chi - clo], U32, "z_codes%d" % c)
                    z_scales = held([P, chi - clo], U8, "z_scales%d" % c)
                    nc.vector.quantize_mx(out=z_codes[:].bitcast(FP8X4), scales=z_scales[:], in_=woven[:])
                    for u in range(PACK):
                        product(h_banks[c][u], w2_dealt, u, z_codes[:], z_scales[:])

        for t, lo, hi in PIECES:
            part, diff = hinge_front(t, lo, hi)
            hinge_back(t, lo, hi, part, diff)

        for t in range(PACK):
            for c in range(len(CHUNKS)):
                on_vector = t == 0 and c == len(CHUNKS) - 1
                leave_bank(nc.vector.tensor_copy if on_vector else nc.scalar.copy, "n3", t, CHUNKS[c][0], CHUNKS[c][1], h_banks[c][t])

        out_rows = out_0.rearrange("(p t) j -> p t j", t=PACK)
        out_words = out_1[0].rearrange("p c r -> p (c r)").bitcast(I32)
        result = held([P, PACK, S], F32, "result")
        o_scales = held([P, S], U8, "o_scales")
        inverses = []

        def denominator(t):
            d4 = less_self("n4", t, 0, S)
            size = work.tile([P, S], F32, name="size")
            nc.scalar.activation(size[:], d4[:], ACT.Abs)
            root = work.tile([P, S], F32, name="root")
            nc.scalar.activation(root[:], size[:], ACT.Abs_reciprocal_sqrt, bias=0.5)
            inverse = held([P, S], F32, "inverse%d" % t)
            nc.scalar.activation(inverse[:], root[:], ACT.Square)
            inverses.append(inverse)

        denominator(0)
        for t, lo, hi in OUT_PIECES:
            if lo == 0 and t + 1 < PACK:
                denominator(t + 1)
            d3 = less_self("n3", t, lo, hi)
            nc.vector.scalar_tensor_tensor(result[:, t, lo:hi], d3[:], -1.0, inverses[t][:, lo:hi], ALU.mult, ALU.mult)
            nc.sync.dma_start(out_rows[:, t, lo:hi], result[:, t, lo:hi])
            if t == PACK - 1:
                woven = held([P, PACK * HALF], BF16, "o_woven%d" % lo)
                weave(nc.vector.tensor_copy if hi == S else nc.scalar.copy, woven, result[:, :, lo:hi])
                o_codes = held([P, HALF], I32, "o_codes%d" % lo)
                nc.vector.quantize_mx(out=o_codes[:].bitcast(FP8X4), scales=o_scales[:, lo:hi], in_=woven[:])
                nc.scalar.dma_start(out_words[:, lo:hi], o_codes[:])
        for q in range(4):
            queue = nc.sync if q % 2 == 0 else nc.scalar
            queue.dma_start(out_2[0, 4 * q : 4 * q + 4, :].bitcast(I32), o_scales[32 * q : 32 * q + 4, :].bitcast(I32))
